import numpy as np
import ml_dtypes


def mxq(x, axis, fmt="e4m3"):
    dtype, down = {"e4m3": (ml_dtypes.float8_e4m3fn, 7), "e5m2": (ml_dtypes.float8_e5m2, 14)}[fmt]
    v = np.moveaxis(np.asarray(x, np.float32).astype(ml_dtypes.bfloat16).astype(np.float64), axis, -1)
    blocks = v.reshape(v.shape[:-1] + (-1, 32))
    amax = np.abs(blocks).max(-1, keepdims=True)
    byte = np.maximum(np.where(amax > 0, np.frexp(amax)[1] - 1 + 127, 0) - down, 1)
    scale = np.exp2(byte - 127.0)
    codes = (blocks / scale).astype(np.float32).astype(dtype).astype(np.float64)
    return np.moveaxis((codes * scale).reshape(v.shape), -1, axis)


WIDE = False


def mx_kscale(k):
    if not WIDE:
        return np.ones(k)
    levels = np.array([24, -24, 12, -12, 0])
    if k % 512:
        return np.exp2(np.random.permutation(np.resize(levels, k // 32))).repeat(32)
    a = np.empty((k // 512, 16))
    for p in range(k // 512):
        a[p, :8] = np.random.permutation(np.resize(levels, 8))
        for g in range(8):
            far = levels[np.abs(levels - a[p, g]) >= 10]
            a[p, g + 8] = far[np.random.randint(len(far))]
    return np.exp2(a.ravel()).repeat(32)


def f64(x):
    return np.asarray(x).astype(np.float64)


def striped8(idx):
    return np.concatenate([v.reshape(-1, 16).T for v in idx]).astype(np.uint16)


def unstriped8(offs):
    return np.stack([offs[16 * g:16 * g + 16].T.reshape(-1) for g in range(8)]).astype(np.int64)


K, L, N, T, J = 1024, 512, 512, 2048, 1024


def setup_inputs():
    n = np.random.standard_normal
    s = mx_kscale(K)[:, None]
    return {
        "xT": (n((K, T)) * s).astype(np.float32),
        "wgt": np.repeat(np.random.uniform(0.5, 2.0, (8, J)), 16, axis=0).astype(np.float32),
        "wt": (n((K, N)) / np.sqrt(K) / s).astype(np.float32),
        "res": (n((N, J))).astype(np.float32),
        "offs": striped8(np.stack([np.random.permutation(T)[:J] for _ in range(8)])),
    }


def reference(xT, wgt, wt, res, offs):
    idx = unstriped8(offs)
    rows = np.arange(K)
    xg = f64(wgt)[rows // 4 % 128] * f64(xT)[rows[:, None], idx[rows % 512 // 64]]
    xT_ = mxq(xg, 0, "e4m3")
    wt_q_ = mxq(f64(wt), 0, "e4m3")
    wt_r_ = mxq(f64(wt) - wt_q_, 0, "e4m3")
    y = wt_q_.T @ xT_ + wt_r_.T @ xT_
    return f64(res) + y

@@ -1,0 +1,217 @@
+from contextlib import ExitStack
+
+import concourse.mybir as mybir
+from concourse.masks import make_identity
+
+K, N, T, J = 1024, 512, 2048, 1024
+FLOPS = 2 * 2 * K * N * J + 2 * 512 * K * N
+
+F32 = mybir.dt.float32
+BF16 = mybir.dt.bfloat16
+U32 = mybir.dt.uint32
+U16 = mybir.dt.uint16
+U8 = mybir.dt.uint8
+FP8X4 = mybir.dt.float8_e4m3fn_x4
+MULT = mybir.AluOpType.mult
+ADD = mybir.AluOpType.add
+SUB = mybir.AluOpType.subtract
+
+P = 128
+PACK = 4
+K_PASS = P * PACK
+PASSES = K // K_PASS
+N_BLOCKS = N // P
+BANK = 512
+CHUNKS = ((0, 512), (512, 256), (768, 256))
+RUN = 2
+
+
+def by_planes(ap):
+    return ap.rearrange("p i (c e) -> p c i e", e=RUN)
+
+
+def by_words(ap):
+    return ap.rearrange("p (c e) i -> p c i e", e=RUN)
+
+
+def quantize(nc, codes, scales, woven):
+    nc.vector.quantize_mx(out=codes.bitcast(FP8X4), scales=scales, in_=woven.rearrange("p c i -> p (c i)"))
+
+
+def tile_list_tier_no_res_kernel(tc, xT, wgt, wt, res, offs, out):
+    nc = tc.nc
+    with ExitStack() as ctx:
+        held = ctx.enter_context(tc.tile_pool(name="held", bufs=1))
+        psum = ctx.enter_context(tc.psum_pool(name="psum", bufs=1))
+
+        def sb(shape, dtype, name, tag=None):
+            return held.tile(shape, dtype, name=name, tag=tag or name, align_bytes=64)
+
+        offsets = held.tile([P, J // 16], U16, name="offsets")
+
+        eye = sb([P, P], BF16, "eye")
+        make_identity(nc, eye[:])
+        eye_woven = sb([P, PACK * P, PACK], BF16, "eye_woven")
+        nc.vector.memset(eye_woven[:], 0.0)
+        for i in range(PACK):
+            nc.vector.tensor_copy(out=eye_woven[:, i * P : (i + 1) * P, i], in_=eye[:])
+        eye_codes = sb([P, PACK * P], U32, "eye_codes")
+        eye_scales = sb([P, PACK * P], U8, "eye_scales")
+        quantize(nc, eye_codes[:], eye_scales[:], eye_woven[:])
+
+        half = N // 2
+        w_raw = {}
+        x_plane = {}
+        gate = {}
+        resid = {}
+
+        def load_w(a, h):
+            w_raw[a, h] = sb([P, PACK, half], F32, f"w_raw{a}{h}")
+            rows = wt[a * K_PASS : (a + 1) * K_PASS, h * half : (h + 1) * half]
+            nc.sync.dma_start(out=w_raw[a, h][:], in_=rows.rearrange("(p i) n -> p i n", i=PACK))
+
+        def load_x(a, i):
+            x_plane[a, i] = sb([P, T], F32, f"x{a}{i}")
+            rows = xT[a * K_PASS : (a + 1) * K_PASS, :].rearrange("(p i) t -> p i t", i=PACK)
+            nc.sync.dma_start(out=x_plane[a, i][:], in_=rows[:, i, :])
+
+        def load_gate(c):
+            j0, width = CHUNKS[c]
+            gate[c] = sb([P, width], F32, f"gate{c}")
+            nc.sync.dma_start(out=gate[c][:], in_=wgt[:, j0 : j0 + width])
+
+        def load_res(c):
+            j0, width = CHUNKS[c]
+            resid[c] = sb([P, N_BLOCKS, width], F32, f"res{c}")
+            nc.sync.dma_start(out=resid[c][:], in_=res[:, j0 : j0 + width].rearrange("(b p) j -> p b j", p=P))
+
+        load_w(0, 0)
+        load_w(0, 1)
+        nc.sync.dma_start(offsets[:], offs)
+        load_gate(0)
+        load_x(0, 0)
+        load_gate(1)
+        load_gate(2)
+        load_x(0, 1)
+        load_x(0, 2)
+        load_w(1, 0)
+        load_w(1, 1)
+        load_x(0, 3)
+        for i in range(PACK):
+            load_x(1, i)
+        for c in range(len(CHUNKS)):
+            load_res(c)
+
+        tiers = {}
+
+        def make_tiers(a):
+            q_codes = sb([P, N], U32, f"q_codes{a}")
+            q_scales = sb([P, N], U8, f"q_scales{a}")
+            r_codes = sb([P, N], U32, f"r_codes{a}")
+            r_scales = sb([P, N], U8, f"r_scales{a}")
+            r_woven = sb([P, N, PACK], BF16, f"r_woven{a}")
+            for h in range(2):
+                q_woven = sb([P, half, PACK], BF16, f"q_woven{a}{h}")
+                nc.scalar.copy(out=by_words(q_woven[:]), in_=by_planes(w_raw[a, h][:]))
+                cols = slice(h * half, (h + 1) * half)
+                quantize(nc, q_codes[:, cols], q_scales[:, cols], q_woven[:])
+            for b in range(N_BLOCKS):
+                cols = slice(b * P, (b + 1) * P)
+                back = psum.tile([P, PACK, P], F32, name=f"back{a}{b}", tag=f"bank{N_BLOCKS + b}")
+                for i in range(PACK):
+                    rows = slice(i * P, (i + 1) * P)
+                    nc.tensor.matmul_mx(
+                        out=back[:, i, :],
+                        lhsT=eye_codes[:, rows].bitcast(FP8X4),
+                        lhsT_scale=eye_scales[:, rows],
+                        rhs=q_codes[:, cols].bitcast(FP8X4),
+                        rhs_scale=q_scales[:, cols],
+                        start=True,
+                        stop=True,
+                    )
+                h, b_in = divmod(b, 2)
+                nc.vector.tensor_tensor(
+                    out=by_words(r_woven[:, cols, :]),
+                    in0=by_planes(w_raw[a, h][:, :, b_in * P : (b_in + 1) * P]),
+                    in1=by_planes(back[:]),
+                    op=SUB,
+                )
+            quantize(nc, r_codes[:], r_scales[:], r_woven[:])
+            tiers[a] = ((q_codes, q_scales), (r_codes, r_scales))
+
+        picked = {}
+        xg = {}
+
+        def gather(a, i, c, tag=None):
+            j0, width = CHUNKS[c]
+            if i == 0:
+                picked[a, c] = sb([P, PACK, width], F32, f"picked{a}{c}", tag)
+            nc.vector.tensor_tensor(
+                out=picked[a, c][:, i, :],
+                in0=x_plane[a, i][:].indirect(offsets[:, j0 // 16 : (j0 + width) // 16]),
+                in1=gate[c][:],
+                op=MULT,
+            )
+
+        def quantize_x(a, c):
+            width = CHUNKS[c][1]
+            woven = sb([P, width, PACK], BF16, f"x_woven{a}{c}")
+            nc.scalar.copy(out=by_words(woven[:]), in_=by_planes(picked[a, c][:]))
+            codes = sb([P, width], U32, f"x_codes{a}{c}")
+            scales = sb([P, width], U8, f"x_scales{a}{c}")
+            quantize(nc, codes[:], scales[:], woven[:])
+            xg[a, c] = (codes, scales)
+
+        sums = {}
+        first_bank = (0, 4, 6)
+
+        def multiply(a, c):
+            width = CHUNKS[c][1]
+            share = BANK // width
+            x_codes, x_scales = xg[a, c]
+            for g in range(N_BLOCKS // share):
+                if a == 0:
+                    sums[c, g] = psum.tile([P, share, width], F32, name=f"sum{c}{g}", tag=f"bank{first_bank[c] + g}")
+                for s in range(share):
+                    cols = slice((g * share + s) * P, (g * share + s + 1) * P)
+                    for tier in range(2):
+                        w_codes, w_scales = tiers[a][tier]
+                        nc.tensor.matmul_mx(
+                            out=sums[c, g][:, s, :],
+                            lhsT=w_codes[:, cols].bitcast(FP8X4),
+                            lhsT_scale=w_scales[:, cols],
+                            rhs=x_codes[:].bitcast(FP8X4),
+                            rhs_scale=x_scales[:],
+                            start=(a == 0 and s == 0 and tier == 0),
+                            stop=(a == PASSES - 1 and s == share - 1 and tier == 1),
+                        )
+
+        def finish(c):
+            j0, width = CHUNKS[c]
+            share = BANK // width
+            for g in range(N_BLOCKS // share):
+                total = sb([P, share, width], F32, f"total{c}{g}")
+                nc.vector.tensor_tensor(
+                    out=total[:], in0=sums[c, g][:], in1=resid[c][:, g * share : (g + 1) * share, :], op=ADD
+                )
+                rows = out[g * share * P : (g + 1) * share * P, j0 : j0 + width]
+                nc.sync.dma_start(out=rows.rearrange("(b p) j -> p b j", p=P), in_=total[:])
+
+        make_tiers(0)
+        for i in range(PACK - 1):
+            for c in range(len(CHUNKS)):
+                gather(0, i, c)
+        make_tiers(1)
+        for c in range(len(CHUNKS)):
+            gather(0, PACK - 1, c)
+            quantize_x(0, c)
+            multiply(0, c)
+
+        order_tags = (None, "gate0", "x_woven10")
+        for c in range(len(CHUNKS)):
+            for i in range(PACK):
+                gather(1, i, c, order_tags[c])
+            quantize_x(1, c)
+            multiply(1, c)
+        for c in range(len(CHUNKS)):
+            finish(c)

@@ -1,7 +1,6 @@
 from contextlib import ExitStack
 
 import concourse.mybir as mybir
-from concourse.masks import make_identity
 
 K, N, T, J = 1024, 512, 2048, 1024
 FLOPS = 2 * 2 * K * N * J + 2 * 512 * K * N
@@ -15,15 +14,24 @@ FP8X4 = mybir.dt.float8_e4m3fn_x4
 MULT = mybir.AluOpType.mult
 ADD = mybir.AluOpType.add
 SUB = mybir.AluOpType.subtract
+EQUAL = mybir.AluOpType.is_equal
 
 P = 128
 PACK = 4
+QUAD = 32
 K_PASS = P * PACK
 PASSES = K // K_PASS
 N_BLOCKS = N // P
 BANK = 512
-CHUNKS = ((0, 512), (512, 256), (768, 256))
+HALF = J // 2
+CHUNKS = ((0, 256), (256, 256), (512, 256), (768, 256))
+FIRST_BANK = (0, 2, 4, 6)
 RUN = 2
+ON_TENSOR = ((1, 0), (1, 1), (1, 2), (1, 3))
+LOADS = (("w", 0, 0), ("w", 0, 1), ("o",), ("g", 0), ("x", 0, 0), ("w", 1, 0), ("w", 1, 1), ("x", 0, 1), ("x", 0, 2), ("x", 0, 3), ("x", 1, 0), ("x", 1, 1), ("x", 1, 2), ("x", 1, 3))
+ORDER_TAGS = "x_woven10"
+WOVEN_TAGS = {}
+PICKED0_TAG = "w_raw01"
 
 
 def by_planes(ap):
@@ -42,6 +50,7 @@ def tile_list_tier_no_res_kernel(tc, xT, wgt, wt, res, offs, out):
     nc = tc.nc
     with ExitStack() as ctx:
         held = ctx.enter_context(tc.tile_pool(name="held", bufs=1))
+        ring = ctx.enter_context(tc.tile_pool(name="ring", bufs=2))
         psum = ctx.enter_context(tc.psum_pool(name="psum", bufs=1))
 
         def sb(shape, dtype, name, tag=None):
@@ -49,20 +58,34 @@ def tile_list_tier_no_res_kernel(tc, xT, wgt, wt, res, offs, out):
 
         offsets = held.tile([P, J // 16], U16, name="offsets")
 
-        eye = sb([P, P], BF16, "eye")
-        make_identity(nc, eye[:])
-        eye_woven = sb([P, PACK * P, PACK], BF16, "eye_woven")
-        nc.vector.memset(eye_woven[:], 0.0)
-        for i in range(PACK):
-            nc.vector.tensor_copy(out=eye_woven[:, i * P : (i + 1) * P, i], in_=eye[:])
+        ones = sb([P, QUAD], F32, "ones")
+        nc.vector.memset(ones[:], 1.0)
+        eye = sb([P, P], F32, "eye")
+        nc.vector.memset(eye[:], 0.0)
+        column = sb([P, QUAD], F32, "column")
+        nc.vector.tensor_tensor_scan(out=column[:], data0=ones[:], data1=ones[:], initial=0.0, op0=MULT, op1=ADD)
+        eye_woven = [sb([P, P, PACK], BF16, f"eye_woven{i}") for i in range(PACK)]
+        nc.vector.memset(eye_woven[0][:].bitcast(U32), 0)
+        row = sb([P, QUAD], F32, "row")
+        nc.vector.transpose(out=row[:], in_=column[:])
+        for i in range(1, PACK):
+            nc.vector.memset(eye_woven[i][:].bitcast(U32), 0)
+        for q in range(0, P, QUAD):
+            nc.vector.tensor_tensor(
+                out=eye[q : q + QUAD, q : q + QUAD], in0=column[q : q + QUAD, :], in1=row[q : q + QUAD, :], op=EQUAL
+            )
+        nc.scalar.copy(out=eye_woven[PACK - 1][:, :, PACK - 1], in_=eye[:])
+        for i in range(PACK - 1):
+            nc.vector.tensor_copy(out=eye_woven[i][:, :, i], in_=eye[:])
         eye_codes = sb([P, PACK * P], U32, "eye_codes")
         eye_scales = sb([P, PACK * P], U8, "eye_scales")
-        quantize(nc, eye_codes[:], eye_scales[:], eye_woven[:])
+        for i in range(PACK):
+            quantize(nc, eye_codes[:, i * P : (i + 1) * P], eye_scales[:, i * P : (i + 1) * P], eye_woven[i][:])
 
         half = N // 2
         w_raw = {}
         x_plane = {}
-        gate = {}
+        gate = sb([P, J], F32, "gate")
         resid = {}
 
         def load_w(a, h):
@@ -75,49 +98,42 @@ def tile_list_tier_no_res_kernel(tc, xT, wgt, wt, res, offs, out):
             rows = xT[a * K_PASS : (a + 1) * K_PASS, :].rearrange("(p i) t -> p i t", i=PACK)
             nc.sync.dma_start(out=x_plane[a, i][:], in_=rows[:, i, :])
 
-        def load_gate(c):
-            j0, width = CHUNKS[c]
-            gate[c] = sb([P, width], F32, f"gate{c}")
-            nc.sync.dma_start(out=gate[c][:], in_=wgt[:, j0 : j0 + width])
+        def load_gate(h):
+            nc.sync.dma_start(out=gate[:], in_=wgt)
 
         def load_res(c):
             j0, width = CHUNKS[c]
             resid[c] = sb([P, N_BLOCKS, width], F32, f"res{c}")
             nc.sync.dma_start(out=resid[c][:], in_=res[:, j0 : j0 + width].rearrange("(b p) j -> p b j", p=P))
 
-        load_w(0, 0)
-        load_w(0, 1)
-        nc.sync.dma_start(offsets[:], offs)
-        load_gate(0)
-        load_x(0, 0)
-        load_gate(1)
-        load_gate(2)
-        load_x(0, 1)
-        load_x(0, 2)
-        load_w(1, 0)
-        load_w(1, 1)
-        load_x(0, 3)
-        for i in range(PACK):
-            load_x(1, i)
+        for item in LOADS:
+            if item[0] == "o":
+                nc.sync.dma_start(offsets[:], offs)
+            elif item[0] == "w":
+                load_w(item[1], item[2])
+            elif item[0] == "x":
+                load_x(item[1], item[2])
+            else:
+                load_gate(item[1])
         for c in range(len(CHUNKS)):
             load_res(c)
 
         tiers = {}
+        left_over = {}
 
-        def make_tiers(a):
-            q_codes = sb([P, N], U32, f"q_codes{a}")
-            q_scales = sb([P, N], U8, f"q_scales{a}")
-            r_codes = sb([P, N], U32, f"r_codes{a}")
-            r_scales = sb([P, N], U8, f"r_scales{a}")
-            r_woven = sb([P, N, PACK], BF16, f"r_woven{a}")
-            for h in range(2):
-                q_woven = sb([P, half, PACK], BF16, f"q_woven{a}{h}")
-                nc.scalar.copy(out=by_words(q_woven[:]), in_=by_planes(w_raw[a, h][:]))
-                cols = slice(h * half, (h + 1) * half)
-                quantize(nc, q_codes[:, cols], q_scales[:, cols], q_woven[:])
-            for b in range(N_BLOCKS):
-                cols = slice(b * P, (b + 1) * P)
-                back = psum.tile([P, PACK, P], F32, name=f"back{a}{b}", tag=f"bank{N_BLOCKS + b}")
+        def make_tiers(a, h):
+            q_codes = sb([P, half], U32, f"q_codes{a}{h}")
+            q_scales = sb([P, half], U8, f"q_scales{a}{h}")
+            if h == 0:
+                left_over[a] = sb([P, N, PACK], BF16, f"r_woven{a}")
+            r_woven = left_over[a][:, h * half : (h + 1) * half, :]
+            q_woven = sb([P, half, PACK], BF16, f"q_woven{a}{h}", WOVEN_TAGS.get((a, h)))
+            nc.scalar.copy(out=by_words(q_woven[:]), in_=by_planes(w_raw[a, h][:]))
+            quantize(nc, q_codes[:], q_scales[:], q_woven[:])
+            for b_in in range(2):
+                b = 2 * h + b_in
+                cols = slice(b_in * P, (b_in + 1) * P)
+                back = psum.tile([P, PACK, P], F32, name=f"back{a}{b}", tag=f"bank{(N_BLOCKS * a + b) % 3}")
                 for i in range(PACK):
                     rows = slice(i * P, (i + 1) * P)
                     nc.tensor.matmul_mx(
@@ -129,59 +145,70 @@ def tile_list_tier_no_res_kernel(tc, xT, wgt, wt, res, offs, out):
                         start=True,
                         stop=True,
                     )
-                h, b_in = divmod(b, 2)
-                nc.vector.tensor_tensor(
-                    out=by_words(r_woven[:, cols, :]),
-                    in0=by_planes(w_raw[a, h][:, :, b_in * P : (b_in + 1) * P]),
-                    in1=by_planes(back[:]),
-                    op=SUB,
-                )
-            quantize(nc, r_codes[:], r_scales[:], r_woven[:])
-            tiers[a] = ((q_codes, q_scales), (r_codes, r_scales))
+                if (a, b) in ON_TENSOR:
+                    minus = ring.tile([P, PACK, P], F32, name="minus", tag="minus")
+                    nc.scalar.mul(minus[:], back[:], -1.0)
+                    left = psum.tile([P, PACK, P], F32, name=f"left{a}{b}", tag=f"bank{3 + (N_BLOCKS * a + b) % 3}")
+                    for i in range(PACK):
+                        nc.tensor.matmul(left[:, i, :], lhsT=w_raw[a, h][:, i, cols], rhs=eye[:], is_transpose=True, start=True, stop=False)
+                        nc.tensor.matmul(left[:, i, :], lhsT=minus[:, i, :], rhs=eye[:], is_transpose=True, start=False, stop=True)
+                    pairs = ring.tile([P, 2, P, 2], BF16, name="pairs", tag="pairs")
+                    nc.scalar.copy(out=pairs[:], in_=left[:].rearrange("n (u e) p -> n u p e", e=2))
+                    words = pairs[:].rearrange("n u p e -> n (u p e)").bitcast(F32)
+                    turned = psum.tile([P, 2, P], F32, name=f"turned{a}{b}", tag=f"bank{6 + b % 2}")
+                    for u in range(2):
+                        nc.tensor.transpose(turned[:, u, :], words[:, u * P : (u + 1) * P], eye[:])
+                    nc.scalar.copy(out=r_woven[:, cols, :].bitcast(F32), in_=turned[:].rearrange("p u n -> p n u"))
+                else:
+                    nc.vector.tensor_tensor(
+                        out=by_words(r_woven[:, cols, :]),
+                        in0=by_planes(w_raw[a, h][:, :, cols]),
+                        in1=by_planes(back[:]),
+                        op=SUB,
+                    )
+            tiers[a, h, 0] = (q_codes[:], q_scales[:])
+            if h == 1:
+                r_codes = sb([P, N], U32, f"r_codes{a}")
+                r_scales = sb([P, N], U8, f"r_scales{a}")
+                quantize(nc, r_codes[:], r_scales[:], left_over[a][:])
+                for k in range(2):
+                    tiers[a, k, 1] = (r_codes[:, k * half : (k + 1) * half], r_scales[:, k * half : (k + 1) * half])
 
-        picked = {}
-        xg = {}
-
-        def gather(a, i, c, tag=None):
-            j0, width = CHUNKS[c]
-            if i == 0:
-                picked[a, c] = sb([P, PACK, width], F32, f"picked{a}{c}", tag)
+        def gather(dst, a, i, j0, width):
             nc.vector.tensor_tensor(
-                out=picked[a, c][:, i, :],
+                out=dst,
                 in0=x_plane[a, i][:].indirect(offsets[:, j0 // 16 : (j0 + width) // 16]),
-                in1=gate[c][:],
+                in1=gate[:, j0 : j0 + width],
                 op=MULT,
             )
 
-        def quantize_x(a, c):
-            width = CHUNKS[c][1]
-            woven = sb([P, width, PACK], BF16, f"x_woven{a}{c}")
-            nc.scalar.copy(out=by_words(woven[:]), in_=by_planes(picked[a, c][:]))
-            codes = sb([P, width], U32, f"x_codes{a}{c}")
-            scales = sb([P, width], U8, f"x_scales{a}{c}")
+        def quantize_x(picked, width, name):
+            woven = sb([P, width, PACK], BF16, f"x_woven{name}")
+            nc.scalar.copy(out=by_words(woven[:]), in_=by_planes(picked))
+            codes = sb([P, width], U32, f"x_codes{name}")
+            scales = sb([P, width], U8, f"x_scales{name}")
             quantize(nc, codes[:], scales[:], woven[:])
-            xg[a, c] = (codes, scales)
+            return codes, scales
 
         sums = {}
-        first_bank = (0, 4, 6)
 
-        def multiply(a, c):
+        def multiply(a, c, x_codes, x_scales):
             width = CHUNKS[c][1]
             share = BANK // width
-            x_codes, x_scales = xg[a, c]
             for g in range(N_BLOCKS // share):
                 if a == 0:
-                    sums[c, g] = psum.tile([P, share, width], F32, name=f"sum{c}{g}", tag=f"bank{first_bank[c] + g}")
+                    sums[c, g] = psum.tile([P, share, width], F32, name=f"sum{c}{g}", tag=f"bank{FIRST_BANK[c] + g}")
                 for s in range(share):
-                    cols = slice((g * share + s) * P, (g * share + s + 1) * P)
+                    h, b_in = divmod(g * share + s, 2)
+                    cols = slice(b_in * P, (b_in + 1) * P)
                     for tier in range(2):
-                        w_codes, w_scales = tiers[a][tier]
+                        w_codes, w_scales = tiers[a, h, tier]
                         nc.tensor.matmul_mx(
                             out=sums[c, g][:, s, :],
                             lhsT=w_codes[:, cols].bitcast(FP8X4),
                             lhsT_scale=w_scales[:, cols],
-                            rhs=x_codes[:].bitcast(FP8X4),
-                            rhs_scale=x_scales[:],
+                            rhs=x_codes.bitcast(FP8X4),
+                            rhs_scale=x_scales,
                             start=(a == 0 and s == 0 and tier == 0),
                             stop=(a == PASSES - 1 and s == share - 1 and tier == 1),
                         )
@@ -197,21 +224,35 @@ def tile_list_tier_no_res_kernel(tc, xT, wgt, wt, res, offs, out):
                 rows = out[g * share * P : (g + 1) * share * P, j0 : j0 + width]
                 nc.sync.dma_start(out=rows.rearrange("(b p) j -> p b j", p=P), in_=total[:])
 
-        make_tiers(0)
-        for i in range(PACK - 1):
-            for c in range(len(CHUNKS)):
-                gather(0, i, c)
-        make_tiers(1)
-        for c in range(len(CHUNKS)):
-            gather(0, PACK - 1, c)
-            quantize_x(0, c)
-            multiply(0, c)
+        make_tiers(0, 0)
+        make_tiers(0, 1)
+        picked = sb([P, PACK, J], F32, "picked0", PICKED0_TAG)
+        gather(picked[:, 0, :], 0, 0, 0, J)
+        make_tiers(1, 0)
+        make_tiers(1, 1)
+        for i in range(1, PACK):
+            gather(picked[:, i, :], 0, i, 0, J)
+        for h in range(2):
+            codes, scales = quantize_x(picked[:, :, h * HALF : (h + 1) * HALF], HALF, f"0{h}")
+            for c in (2 * h, 2 * h + 1):
+                j0, width = CHUNKS[c]
+                cols = slice(j0 % HALF, j0 % HALF + width)
+                multiply(0, c, codes[:, cols], scales[:, cols])
 
-        order_tags = (None, "gate0", "x_woven10")
-        for c in range(len(CHUNKS)):
+        for c in range(2):
+            j0, width = CHUNKS[c]
+            piece = sb([P, PACK, width], F32, f"picked1{c}")
             for i in range(PACK):
-                gather(1, i, c, order_tags[c])
-            quantize_x(1, c)
-            multiply(1, c)
-        for c in range(len(CHUNKS)):
-            finish(c)
+                gather(piece[:, i, :], 1, i, j0, width)
+            codes, scales = quantize_x(piece[:], width, f"1{c}")
+            multiply(1, c, codes[:], scales[:])
+        piece = sb([P, PACK, HALF], F32, "picked12", ORDER_TAGS)
+        for i in range(PACK):
+            gather(piece[:, i, :], 1, i, HALF, HALF)
+        for c in range(2, 4):
+            j0, width = CHUNKS[c]
+            codes, scales = quantize_x(piece[:, :, j0 - HALF : j0 - HALF + width], width, f"1{c}")
+            multiply(1, c, codes[:], scales[:])
+            finish(c - 2)
+        finish(2)
+        finish(3)

@@ -19,27 +19,22 @@ EQUAL = mybir.AluOpType.is_equal
 P = 128
 PACK = 4
 QUAD = 32
+LIST_ROWS = 16
 K_PASS = P * PACK
 PASSES = K // K_PASS
-N_BLOCKS = N // P
-BANK = 512
-HALF = J // 2
-CHUNKS = ((0, 256), (256, 256), (512, 256), (768, 256))
-FIRST_BANK = (0, 2, 4, 6)
+W_HALF = N // 2
+J_HALF = J // 2
+CHUNK = 256
+CHUNKS = J // CHUNK
 RUN = 2
-ON_TENSOR = ((1, 0), (1, 1), (1, 2), (1, 3))
-LOADS = (("w", 0, 0), ("w", 0, 1), ("o",), ("g", 0), ("x", 0, 0), ("w", 1, 0), ("w", 1, 1), ("x", 0, 1), ("x", 0, 2), ("x", 0, 3), ("x", 1, 0), ("x", 1, 1), ("x", 1, 2), ("x", 1, 3))
-ORDER_TAGS = "x_woven10"
-WOVEN_TAGS = {}
-PICKED0_TAG = "w_raw01"
 
 
-def by_planes(ap):
-    return ap.rearrange("p i (c e) -> p c i e", e=RUN)
+def by_planes(planes):
+    return planes.rearrange("p i (c e) -> p c i e", e=RUN)
 
 
-def by_words(ap):
-    return ap.rearrange("p (c e) i -> p c i e", e=RUN)
+def by_words(woven):
+    return woven.rearrange("p (c e) i -> p c i e", e=RUN)
 
 
 def quantize(nc, codes, scales, woven):
@@ -56,7 +51,10 @@ def tile_list_tier_no_res_kernel(tc, xT, wgt, wt, res, offs, out):
         def sb(shape, dtype, name, tag=None):
             return held.tile(shape, dtype, name=name, tag=tag or name, align_bytes=64)
 
-        offsets = held.tile([P, J // 16], U16, name="offsets")
+        def bank(shape, name, number):
+            return psum.tile(shape, F32, name=name, tag=f"bank{number}")
+
+        offsets = held.tile([P, J // LIST_ROWS], U16, name="offsets")
 
         ones = sb([P, QUAD], F32, "ones")
         nc.vector.memset(ones[:], 1.0)
@@ -82,103 +80,109 @@ def tile_list_tier_no_res_kernel(tc, xT, wgt, wt, res, offs, out):
         for i in range(PACK):
             quantize(nc, eye_codes[:, i * P : (i + 1) * P], eye_scales[:, i * P : (i + 1) * P], eye_woven[i][:])
 
-        half = N // 2
-        w_raw = {}
+        w_planes = {}
         x_plane = {}
-        gate = sb([P, J], F32, "gate")
-        resid = {}
+        gate = {}
 
         def load_w(a, h):
-            w_raw[a, h] = sb([P, PACK, half], F32, f"w_raw{a}{h}")
-            rows = wt[a * K_PASS : (a + 1) * K_PASS, h * half : (h + 1) * half]
-            nc.sync.dma_start(out=w_raw[a, h][:], in_=rows.rearrange("(p i) n -> p i n", i=PACK))
+            w_planes[a, h] = sb([P, PACK, W_HALF], F32, f"w_planes{a}{h}")
+            rows = wt[a * K_PASS : (a + 1) * K_PASS, h * W_HALF : (h + 1) * W_HALF]
+            nc.sync.dma_start(out=w_planes[a, h][:], in_=rows.rearrange("(p i) n -> p i n", i=PACK))
 
         def load_x(a, i):
-            x_plane[a, i] = sb([P, T], F32, f"x{a}{i}")
+            x_plane[a, i] = sb([P, T], F32, f"x_plane{a}{i}")
             rows = xT[a * K_PASS : (a + 1) * K_PASS, :].rearrange("(p i) t -> p i t", i=PACK)
             nc.sync.dma_start(out=x_plane[a, i][:], in_=rows[:, i, :])
 
         def load_gate(h):
-            nc.sync.dma_start(out=gate[:], in_=wgt)
+            gate[h] = sb([P, J_HALF], F32, f"gate{h}")
+            nc.sync.dma_start(out=gate[h][:], in_=wgt[:, h * J_HALF : (h + 1) * J_HALF])
 
-        def load_res(c):
-            j0, width = CHUNKS[c]
-            resid[c] = sb([P, N_BLOCKS, width], F32, f"res{c}")
-            nc.sync.dma_start(out=resid[c][:], in_=res[:, j0 : j0 + width].rearrange("(b p) j -> p b j", p=P))
-
-        for item in LOADS:
-            if item[0] == "o":
-                nc.sync.dma_start(offsets[:], offs)
-            elif item[0] == "w":
-                load_w(item[1], item[2])
-            elif item[0] == "x":
-                load_x(item[1], item[2])
-            else:
-                load_gate(item[1])
-        for c in range(len(CHUNKS)):
-            load_res(c)
+        for a in range(PASSES):
+            for h in range(2):
+                load_w(a, h)
+        nc.sync.dma_start(offsets[:], offs)
+        load_gate(0)
+        load_x(0, 0)
+        load_gate(1)
+        for plane in range(1, PASSES * PACK):
+            load_x(plane // PACK, plane % PACK)
+        residual = sb([P, 2, 2, J], F32, "residual")
+        for h in range(2):
+            rows = res[h * W_HALF : (h + 1) * W_HALF, :]
+            nc.sync.dma_start(out=residual[:, h], in_=rows.rearrange("(s p) j -> p s j", p=P))
 
         tiers = {}
-        left_over = {}
 
-        def make_tiers(a, h):
-            q_codes = sb([P, half], U32, f"q_codes{a}{h}")
-            q_scales = sb([P, half], U8, f"q_scales{a}{h}")
-            if h == 0:
-                left_over[a] = sb([P, N, PACK], BF16, f"r_woven{a}")
-            r_woven = left_over[a][:, h * half : (h + 1) * half, :]
-            q_woven = sb([P, half, PACK], BF16, f"q_woven{a}{h}", WOVEN_TAGS.get((a, h)))
-            nc.scalar.copy(out=by_words(q_woven[:]), in_=by_planes(w_raw[a, h][:]))
-            quantize(nc, q_codes[:], q_scales[:], q_woven[:])
-            for b_in in range(2):
-                b = 2 * h + b_in
-                cols = slice(b_in * P, (b_in + 1) * P)
-                back = psum.tile([P, PACK, P], F32, name=f"back{a}{b}", tag=f"bank{(N_BLOCKS * a + b) % 3}")
-                for i in range(PACK):
-                    rows = slice(i * P, (i + 1) * P)
-                    nc.tensor.matmul_mx(
-                        out=back[:, i, :],
-                        lhsT=eye_codes[:, rows].bitcast(FP8X4),
-                        lhsT_scale=eye_scales[:, rows],
-                        rhs=q_codes[:, cols].bitcast(FP8X4),
-                        rhs_scale=q_scales[:, cols],
-                        start=True,
-                        stop=True,
-                    )
-                if (a, b) in ON_TENSOR:
-                    minus = ring.tile([P, PACK, P], F32, name="minus", tag="minus")
-                    nc.scalar.mul(minus[:], back[:], -1.0)
-                    left = psum.tile([P, PACK, P], F32, name=f"left{a}{b}", tag=f"bank{3 + (N_BLOCKS * a + b) % 3}")
-                    for i in range(PACK):
-                        nc.tensor.matmul(left[:, i, :], lhsT=w_raw[a, h][:, i, cols], rhs=eye[:], is_transpose=True, start=True, stop=False)
-                        nc.tensor.matmul(left[:, i, :], lhsT=minus[:, i, :], rhs=eye[:], is_transpose=True, start=False, stop=True)
-                    pairs = ring.tile([P, 2, P, 2], BF16, name="pairs", tag="pairs")
-                    nc.scalar.copy(out=pairs[:], in_=left[:].rearrange("n (u e) p -> n u p e", e=2))
-                    words = pairs[:].rearrange("n u p e -> n (u p e)").bitcast(F32)
-                    turned = psum.tile([P, 2, P], F32, name=f"turned{a}{b}", tag=f"bank{6 + b % 2}")
-                    for u in range(2):
-                        nc.tensor.transpose(turned[:, u, :], words[:, u * P : (u + 1) * P], eye[:])
-                    nc.scalar.copy(out=r_woven[:, cols, :].bitcast(F32), in_=turned[:].rearrange("p u n -> p n u"))
-                else:
-                    nc.vector.tensor_tensor(
-                        out=by_words(r_woven[:, cols, :]),
-                        in0=by_planes(w_raw[a, h][:, :, cols]),
-                        in1=by_planes(back[:]),
-                        op=SUB,
-                    )
-            tiers[a, h, 0] = (q_codes[:], q_scales[:])
-            if h == 1:
-                r_codes = sb([P, N], U32, f"r_codes{a}")
-                r_scales = sb([P, N], U8, f"r_scales{a}")
-                quantize(nc, r_codes[:], r_scales[:], left_over[a][:])
-                for k in range(2):
-                    tiers[a, k, 1] = (r_codes[:, k * half : (k + 1) * half], r_scales[:, k * half : (k + 1) * half])
+        def first_tier(a, h):
+            codes = sb([P, W_HALF], U32, f"q_codes{a}{h}")
+            scales = sb([P, W_HALF], U8, f"q_scales{a}{h}")
+            woven = sb([P, W_HALF, PACK], BF16, f"q_woven{a}{h}")
+            nc.scalar.copy(out=by_words(woven[:]), in_=by_planes(w_planes[a, h][:]))
+            quantize(nc, codes[:], scales[:], woven[:])
+            tiers[a, h, 0] = (codes[:], scales[:])
 
-        def gather(dst, a, i, j0, width):
+        def read_back(a, h, s):
+            codes, scales = tiers[a, h, 0]
+            cols = slice(s * P, (s + 1) * P)
+            back = bank([P, PACK, P], f"back{a}{h}{s}", (4 * a + 2 * h + s) % 3)
+            for i in range(PACK):
+                rows = slice(i * P, (i + 1) * P)
+                nc.tensor.matmul_mx(
+                    out=back[:, i, :],
+                    lhsT=eye_codes[:, rows].bitcast(FP8X4),
+                    lhsT_scale=eye_scales[:, rows],
+                    rhs=codes[:, cols].bitcast(FP8X4),
+                    rhs_scale=scales[:, cols],
+                    start=True,
+                    stop=True,
+                )
+            return back
+
+        def subtract_on_vector(a, h, s, woven):
+            back = read_back(a, h, s)
             nc.vector.tensor_tensor(
-                out=dst,
-                in0=x_plane[a, i][:].indirect(offsets[:, j0 // 16 : (j0 + width) // 16]),
-                in1=gate[:, j0 : j0 + width],
+                out=by_words(woven),
+                in0=by_planes(w_planes[a, h][:, :, s * P : (s + 1) * P]),
+                in1=by_planes(back[:]),
+                op=SUB,
+            )
+
+        def subtract_on_tensor(a, h, s, woven):
+            back = read_back(a, h, s)
+            minus = ring.tile([P, PACK, P], F32, name="minus", tag="minus")
+            nc.scalar.mul(minus[:], back[:], -1.0)
+            left = bank([P, PACK, P], f"left{a}{h}{s}", 3 + (4 * a + 2 * h + s) % 3)
+            for i in range(PACK):
+                plane = w_planes[a, h][:, i, s * P : (s + 1) * P]
+                nc.tensor.matmul(left[:, i, :], lhsT=plane, rhs=eye[:], is_transpose=True, start=True, stop=False)
+                nc.tensor.matmul(left[:, i, :], lhsT=minus[:, i, :], rhs=eye[:], is_transpose=True, start=False, stop=True)
+            pairs = ring.tile([P, 2, P, 2], BF16, name="pairs", tag="pairs")
+            nc.scalar.copy(out=pairs[:], in_=left[:].rearrange("n (u e) p -> n u p e", e=2))
+            words = pairs[:].rearrange("n u p e -> n (u p e)").bitcast(F32)
+            turned = bank([P, 2, P], f"turned{a}{h}{s}", 6 + s)
+            for u in range(2):
+                nc.tensor.transpose(turned[:, u, :], words[:, u * P : (u + 1) * P], eye[:])
+            nc.scalar.copy(out=woven.bitcast(F32), in_=turned[:].rearrange("p u n -> p n u"))
+
+        def second_tier(a, subtract):
+            woven = sb([P, N, PACK], BF16, f"r_woven{a}")
+            for h in range(2):
+                for s in range(2):
+                    first = h * W_HALF + s * P
+                    subtract(a, h, s, woven[:, first : first + P, :])
+            codes = sb([P, N], U32, f"r_codes{a}")
+            scales = sb([P, N], U8, f"r_scales{a}")
+            quantize(nc, codes[:], scales[:], woven[:])
+            for h in range(2):
+                cols = slice(h * W_HALF, (h + 1) * W_HALF)
+                tiers[a, h, 1] = (codes[:, cols], scales[:, cols])
+
+        def gather(picked, a, i, j0, width):
+            nc.vector.tensor_tensor(
+                out=picked[:, i, :],
+                in0=x_plane[a, i][:].indirect(offsets[:, j0 // LIST_ROWS : (j0 + width) // LIST_ROWS]),
+                in1=gate[j0 // J_HALF][:, j0 % J_HALF : j0 % J_HALF + width],
                 op=MULT,
             )
 
@@ -193,66 +197,58 @@ def tile_list_tier_no_res_kernel(tc, xT, wgt, wt, res, offs, out):
         sums = {}
 
         def multiply(a, c, x_codes, x_scales):
-            width = CHUNKS[c][1]
-            share = BANK // width
-            for g in range(N_BLOCKS // share):
+            for h in range(2):
                 if a == 0:
-                    sums[c, g] = psum.tile([P, share, width], F32, name=f"sum{c}{g}", tag=f"bank{FIRST_BANK[c] + g}")
-                for s in range(share):
-                    h, b_in = divmod(g * share + s, 2)
-                    cols = slice(b_in * P, (b_in + 1) * P)
+                    sums[c, h] = bank([P, 2, CHUNK], f"sum{c}{h}", 2 * c + h)
+                for s in range(2):
+                    cols = slice(s * P, (s + 1) * P)
                     for tier in range(2):
                         w_codes, w_scales = tiers[a, h, tier]
                         nc.tensor.matmul_mx(
-                            out=sums[c, g][:, s, :],
+                            out=sums[c, h][:, s, :],
                             lhsT=w_codes[:, cols].bitcast(FP8X4),
                             lhsT_scale=w_scales[:, cols],
                             rhs=x_codes.bitcast(FP8X4),
                             rhs_scale=x_scales,
                             start=(a == 0 and s == 0 and tier == 0),
-                            stop=(a == PASSES - 1 and s == share - 1 and tier == 1),
+                            stop=(a == PASSES - 1 and s == 1 and tier == 1),
                         )
 
         def finish(c):
-            j0, width = CHUNKS[c]
-            share = BANK // width
-            for g in range(N_BLOCKS // share):
-                total = sb([P, share, width], F32, f"total{c}{g}")
-                nc.vector.tensor_tensor(
-                    out=total[:], in0=sums[c, g][:], in1=resid[c][:, g * share : (g + 1) * share, :], op=ADD
-                )
-                rows = out[g * share * P : (g + 1) * share * P, j0 : j0 + width]
-                nc.sync.dma_start(out=rows.rearrange("(b p) j -> p b j", p=P), in_=total[:])
+            total = sb([P, 2, 2, CHUNK], F32, f"total{c}", f"x_woven1{c + 1}" if c + 1 < CHUNKS else None)
+            cols = slice(c * CHUNK, (c + 1) * CHUNK)
+            for h in range(2):
+                nc.vector.tensor_tensor(out=total[:, h], in0=sums[c, h][:], in1=residual[:, h, :, cols], op=ADD)
+                rows = out[h * W_HALF : (h + 1) * W_HALF, cols]
+                nc.sync.dma_start(out=rows.rearrange("(s p) j -> p s j", p=P), in_=total[:, h])
 
-        make_tiers(0, 0)
-        make_tiers(0, 1)
-        picked = sb([P, PACK, J], F32, "picked0", PICKED0_TAG)
-        gather(picked[:, 0, :], 0, 0, 0, J)
-        make_tiers(1, 0)
-        make_tiers(1, 1)
-        for i in range(1, PACK):
-            gather(picked[:, i, :], 0, i, 0, J)
-        for h in range(2):
-            codes, scales = quantize_x(picked[:, :, h * HALF : (h + 1) * HALF], HALF, f"0{h}")
-            for c in (2 * h, 2 * h + 1):
-                j0, width = CHUNKS[c]
-                cols = slice(j0 % HALF, j0 % HALF + width)
-                multiply(0, c, codes[:, cols], scales[:, cols])
+        for a in range(PASSES):
+            for h in range(2):
+                first_tier(a, h)
+        second_tier(0, subtract_on_vector)
+        second_tier(1, subtract_on_tensor)
 
-        for c in range(2):
-            j0, width = CHUNKS[c]
-            piece = sb([P, PACK, width], F32, f"picked1{c}")
-            for i in range(PACK):
-                gather(piece[:, i, :], 1, i, j0, width)
-            codes, scales = quantize_x(piece[:], width, f"1{c}")
-            multiply(1, c, codes[:], scales[:])
-        piece = sb([P, PACK, HALF], F32, "picked12", ORDER_TAGS)
+        picked = sb([P, 2, PACK, J_HALF], F32, "picked0", "q_woven11")
         for i in range(PACK):
-            gather(piece[:, i, :], 1, i, HALF, HALF)
-        for c in range(2, 4):
-            j0, width = CHUNKS[c]
-            codes, scales = quantize_x(piece[:, :, j0 - HALF : j0 - HALF + width], width, f"1{c}")
+            for h in range(2):
+                gather(picked[:, h], 0, i, h * J_HALF, J_HALF)
+        for h in range(2):
+            codes, scales = quantize_x(picked[:, h], J_HALF, f"0{h}")
+            for s in range(2):
+                cols = slice(s * CHUNK, (s + 1) * CHUNK)
+                multiply(0, 2 * h + s, codes[:, cols], scales[:, cols])
+
+        picked = sb([P, PACK, J_HALF], F32, "picked1")
+        for i in range(PACK):
+            gather(picked, 1, i, 0, J_HALF)
+        for c in range(2):
+            codes, scales = quantize_x(picked[:, :, c * CHUNK : (c + 1) * CHUNK], CHUNK, f"1{c}")
             multiply(1, c, codes[:], scales[:])
-            finish(c - 2)
-        finish(2)
-        finish(3)
+        for c, slot in ((2, "gate0"), (3, "x_woven10")):
+            picked = sb([P, PACK, CHUNK], F32, f"picked1{c}", slot)
+            for i in range(PACK):
+                gather(picked, 1, i, c * CHUNK, CHUNK)
+            codes, scales = quantize_x(picked[:], CHUNK, f"1{c}")
+            multiply(1, c, codes[:], scales[:])
+        for c in range(CHUNKS):
+            finish(c)

@@ -84,10 +84,12 @@ def tile_list_tier_no_res_kernel(tc, xT, wgt, wt, res, offs, out):
         x_plane = {}
         gate = {}
 
-        def load_w(a, h):
-            w_planes[a, h] = sb([P, PACK, W_HALF], F32, f"w_planes{a}{h}")
-            rows = wt[a * K_PASS : (a + 1) * K_PASS, h * W_HALF : (h + 1) * W_HALF]
-            nc.sync.dma_start(out=w_planes[a, h][:], in_=rows.rearrange("(p i) n -> p i n", i=PACK))
+        def load_w(a, h0, halves):
+            tile = sb([P, PACK, halves * W_HALF], F32, f"w_planes{a}{h0}")
+            rows = wt[a * K_PASS : (a + 1) * K_PASS, h0 * W_HALF : (h0 + halves) * W_HALF]
+            nc.sync.dma_start(out=tile[:], in_=rows.rearrange("(p i) n -> p i n", i=PACK))
+            for h in range(halves):
+                w_planes[a, h0 + h] = tile[:, :, h * W_HALF : (h + 1) * W_HALF]
 
         def load_x(a, i):
             x_plane[a, i] = sb([P, T], F32, f"x_plane{a}{i}")
@@ -98,9 +100,9 @@ def tile_list_tier_no_res_kernel(tc, xT, wgt, wt, res, offs, out):
             gate[h] = sb([P, J_HALF], F32, f"gate{h}")
             nc.sync.dma_start(out=gate[h][:], in_=wgt[:, h * J_HALF : (h + 1) * J_HALF])
 
-        for a in range(PASSES):
-            for h in range(2):
-                load_w(a, h)
+        load_w(0, 0, 1)
+        load_w(0, 1, 1)
+        load_w(1, 0, 2)
         nc.sync.dma_start(offsets[:], offs)
         load_gate(0)
         load_x(0, 0)
@@ -118,7 +120,7 @@ def tile_list_tier_no_res_kernel(tc, xT, wgt, wt, res, offs, out):
             codes = sb([P, W_HALF], U32, f"q_codes{a}{h}")
             scales = sb([P, W_HALF], U8, f"q_scales{a}{h}")
             woven = sb([P, W_HALF, PACK], BF16, f"q_woven{a}{h}")
-            nc.scalar.copy(out=by_words(woven[:]), in_=by_planes(w_planes[a, h][:]))
+            nc.scalar.copy(out=by_words(woven[:]), in_=by_planes(w_planes[a, h]))
             quantize(nc, codes[:], scales[:], woven[:])
             tiers[a, h, 0] = (codes[:], scales[:])
 
@@ -165,13 +167,16 @@ def tile_list_tier_no_res_kernel(tc, xT, wgt, wt, res, offs, out):
                 nc.tensor.transpose(turned[:, u, :], words[:, u * P : (u + 1) * P], eye[:])
             nc.scalar.copy(out=woven.bitcast(F32), in_=turned[:].rearrange("p u n -> p n u"))
 
-        def second_tier(a, subtract):
+        def left_over(a, subtract):
             woven = sb([P, N, PACK], BF16, f"r_woven{a}")
             for h in range(2):
                 for s in range(2):
                     first = h * W_HALF + s * P
                     subtract(a, h, s, woven[:, first : first + P, :])
-            codes = sb([P, N], U32, f"r_codes{a}")
+            return woven
+
+        def second_tier(a, woven, slot=None):
+            codes = sb([P, N], U32, f"r_codes{a}", slot)
             scales = sb([P, N], U8, f"r_scales{a}")
             quantize(nc, codes[:], scales[:], woven[:])
             for h in range(2):
@@ -225,8 +230,8 @@ def tile_list_tier_no_res_kernel(tc, xT, wgt, wt, res, offs, out):
         for a in range(PASSES):
             for h in range(2):
                 first_tier(a, h)
-        second_tier(0, subtract_on_vector)
-        second_tier(1, subtract_on_tensor)
+        second_tier(0, left_over(0, subtract_on_vector))
+        late_woven = left_over(1, subtract_on_tensor)
 
         picked = sb([P, 2, PACK, J_HALF], F32, "picked0", "q_woven11")
         for i in range(PACK):
@@ -237,6 +242,7 @@ def tile_list_tier_no_res_kernel(tc, xT, wgt, wt, res, offs, out):
             for s in range(2):
                 cols = slice(s * CHUNK, (s + 1) * CHUNK)
                 multiply(0, 2 * h + s, codes[:, cols], scales[:, cols])
+        second_tier(1, late_woven, "x_woven00")
 
         picked = sb([P, PACK, J_HALF], F32, "picked1")
         for i in range(PACK):

from contextlib import ExitStack

import concourse.mybir as mybir

K, N, T, J = 1024, 512, 2048, 1024
FLOPS = 2 * 2 * K * N * J + 2 * 512 * K * N

F32 = mybir.dt.float32
BF16 = mybir.dt.bfloat16
U32 = mybir.dt.uint32
U16 = mybir.dt.uint16
U8 = mybir.dt.uint8
FP8X4 = mybir.dt.float8_e4m3fn_x4
MULT = mybir.AluOpType.mult
ADD = mybir.AluOpType.add
SUB = mybir.AluOpType.subtract
EQUAL = mybir.AluOpType.is_equal

P = 128
PACK = 4
QUAD = 32
LIST_ROWS = 16
K_PASS = P * PACK
PASSES = K // K_PASS
W_HALF = N // 2
J_HALF = J // 2
CHUNK = 256
CHUNKS = J // CHUNK
RUN = 2


def by_planes(planes):
    return planes.rearrange("p i (c e) -> p c i e", e=RUN)


def by_words(woven):
    return woven.rearrange("p (c e) i -> p c i e", e=RUN)


def quantize(nc, codes, scales, woven):
    nc.vector.quantize_mx(out=codes.bitcast(FP8X4), scales=scales, in_=woven.rearrange("p c i -> p (c i)"))


def tile_list_tier_no_res_kernel(tc, xT, wgt, wt, res, offs, out):
    nc = tc.nc
    with ExitStack() as ctx:
        held = ctx.enter_context(tc.tile_pool(name="held", bufs=1))
        ring = ctx.enter_context(tc.tile_pool(name="ring", bufs=2))
        psum = ctx.enter_context(tc.psum_pool(name="psum", bufs=1))

        def sb(shape, dtype, name, tag=None):
            return held.tile(shape, dtype, name=name, tag=tag or name, align_bytes=64)

        def bank(shape, name, number):
            return psum.tile(shape, F32, name=name, tag=f"bank{number}")

        offsets = held.tile([P, J // LIST_ROWS], U16, name="offsets")

        ones = sb([P, QUAD], F32, "ones")
        nc.vector.memset(ones[:], 1.0)
        eye = sb([P, P], F32, "eye")
        nc.vector.memset(eye[:], 0.0)
        column = sb([P, QUAD], F32, "column")
        nc.vector.tensor_tensor_scan(out=column[:], data0=ones[:], data1=ones[:], initial=0.0, op0=MULT, op1=ADD)
        eye_woven = [sb([P, P, PACK], BF16, f"eye_woven{i}") for i in range(PACK)]
        nc.vector.memset(eye_woven[0][:].bitcast(U32), 0)
        row = sb([P, QUAD], F32, "row")
        nc.vector.transpose(out=row[:], in_=column[:])
        for i in range(1, PACK):
            nc.vector.memset(eye_woven[i][:].bitcast(U32), 0)
        for q in range(0, P, QUAD):
            nc.vector.tensor_tensor(
                out=eye[q : q + QUAD, q : q + QUAD], in0=column[q : q + QUAD, :], in1=row[q : q + QUAD, :], op=EQUAL
            )
        nc.scalar.copy(out=eye_woven[PACK - 1][:, :, PACK - 1], in_=eye[:])
        for i in range(PACK - 1):
            nc.vector.tensor_copy(out=eye_woven[i][:, :, i], in_=eye[:])
        eye_codes = sb([P, PACK * P], U32, "eye_codes")
        eye_scales = sb([P, PACK * P], U8, "eye_scales")
        for i in range(PACK):
            quantize(nc, eye_codes[:, i * P : (i + 1) * P], eye_scales[:, i * P : (i + 1) * P], eye_woven[i][:])

        w_planes = {}
        x_plane = {}
        gate = {}

        def load_w(a, h0, halves):
            tile = sb([P, PACK, halves * W_HALF], F32, f"w_planes{a}{h0}")
            rows = wt[a * K_PASS : (a + 1) * K_PASS, h0 * W_HALF : (h0 + halves) * W_HALF]
            nc.sync.dma_start(out=tile[:], in_=rows.rearrange("(p i) n -> p i n", i=PACK))
            for h in range(halves):
                w_planes[a, h0 + h] = tile[:, :, h * W_HALF : (h + 1) * W_HALF]

        def load_x(a, i):
            x_plane[a, i] = sb([P, T], F32, f"x_plane{a}{i}")
            rows = xT[a * K_PASS : (a + 1) * K_PASS, :].rearrange("(p i) t -> p i t", i=PACK)
            nc.sync.dma_start(out=x_plane[a, i][:], in_=rows[:, i, :])

        def load_gate(h):
            gate[h] = sb([P, J_HALF], F32, f"gate{h}")
            nc.sync.dma_start(out=gate[h][:], in_=wgt[:, h * J_HALF : (h + 1) * J_HALF])

        load_w(0, 0, 1)
        load_w(0, 1, 1)
        load_w(1, 0, 2)
        nc.sync.dma_start(offsets[:], offs)
        load_gate(0)
        load_x(0, 0)
        load_gate(1)
        for plane in range(1, PASSES * PACK):
            load_x(plane // PACK, plane % PACK)
        residual = sb([P, 2, 2, J], F32, "residual")
        for h in range(2):
            rows = res[h * W_HALF : (h + 1) * W_HALF, :]
            nc.sync.dma_start(out=residual[:, h], in_=rows.rearrange("(s p) j -> p s j", p=P))

        tiers = {}

        def first_tier(a, h):
            codes = sb([P, W_HALF], U32, f"q_codes{a}{h}")
            scales = sb([P, W_HALF], U8, f"q_scales{a}{h}")
            woven = sb([P, W_HALF, PACK], BF16, f"q_woven{a}{h}")
            nc.scalar.copy(out=by_words(woven[:]), in_=by_planes(w_planes[a, h]))
            quantize(nc, codes[:], scales[:], woven[:])
            tiers[a, h, 0] = (codes[:], scales[:])

        def read_back(a, h, s):
            codes, scales = tiers[a, h, 0]
            cols = slice(s * P, (s + 1) * P)
            back = bank([P, PACK, P], f"back{a}{h}{s}", (4 * a + 2 * h + s) % 3)
            for i in range(PACK):
                rows = slice(i * P, (i + 1) * P)
                nc.tensor.matmul_mx(
                    out=back[:, i, :],
                    lhsT=eye_codes[:, rows].bitcast(FP8X4),
                    lhsT_scale=eye_scales[:, rows],
                    rhs=codes[:, cols].bitcast(FP8X4),
                    rhs_scale=scales[:, cols],
                    start=True,
                    stop=True,
                )
            return back

        def subtract_on_vector(a, h, s, woven):
            back = read_back(a, h, s)
            nc.vector.tensor_tensor(
                out=by_words(woven),
                in0=by_planes(w_planes[a, h][:, :, s * P : (s + 1) * P]),
                in1=by_planes(back[:]),
                op=SUB,
            )

        def subtract_on_tensor(a, h, s, woven):
            back = read_back(a, h, s)
            minus = ring.tile([P, PACK, P], F32, name="minus", tag="minus")
            nc.scalar.mul(minus[:], back[:], -1.0)
            left = bank([P, PACK, P], f"left{a}{h}{s}", 3 + (4 * a + 2 * h + s) % 3)
            for i in range(PACK):
                plane = w_planes[a, h][:, i, s * P : (s + 1) * P]
                nc.tensor.matmul(left[:, i, :], lhsT=plane, rhs=eye[:], is_transpose=True, start=True, stop=False)
                nc.tensor.matmul(left[:, i, :], lhsT=minus[:, i, :], rhs=eye[:], is_transpose=True, start=False, stop=True)
            pairs = ring.tile([P, 2, P, 2], BF16, name="pairs", tag="pairs")
            nc.scalar.copy(out=pairs[:], in_=left[:].rearrange("n (u e) p -> n u p e", e=2))
            words = pairs[:].rearrange("n u p e -> n (u p e)").bitcast(F32)
            turned = bank([P, 2, P], f"turned{a}{h}{s}", 6 + s)
            for u in range(2):
                nc.tensor.transpose(turned[:, u, :], words[:, u * P : (u + 1) * P], eye[:])
            nc.scalar.copy(out=woven.bitcast(F32), in_=turned[:].rearrange("p u n -> p n u"))

        def left_over(a, subtract):
            woven = sb([P, N, PACK], BF16, f"r_woven{a}")
            for h in range(2):
                for s in range(2):
                    first = h * W_HALF + s * P
                    subtract(a, h, s, woven[:, first : first + P, :])
            return woven

        def second_tier(a, woven, slot=None):
            codes = sb([P, N], U32, f"r_codes{a}", slot)
            scales = sb([P, N], U8, f"r_scales{a}")
            quantize(nc, codes[:], scales[:], woven[:])
            for h in range(2):
                cols = slice(h * W_HALF, (h + 1) * W_HALF)
                tiers[a, h, 1] = (codes[:, cols], scales[:, cols])

        def gather(picked, a, i, j0, width):
            nc.vector.tensor_tensor(
                out=picked[:, i, :],
                in0=x_plane[a, i][:].indirect(offsets[:, j0 // LIST_ROWS : (j0 + width) // LIST_ROWS]),
                in1=gate[j0 // J_HALF][:, j0 % J_HALF : j0 % J_HALF + width],
                op=MULT,
            )

        def quantize_x(picked, width, name):
            woven = sb([P, width, PACK], BF16, f"x_woven{name}")
            nc.scalar.copy(out=by_words(woven[:]), in_=by_planes(picked))
            codes = sb([P, width], U32, f"x_codes{name}")
            scales = sb([P, width], U8, f"x_scales{name}")
            quantize(nc, codes[:], scales[:], woven[:])
            return codes, scales

        sums = {}

        def multiply(a, c, x_codes, x_scales):
            for h in range(2):
                if a == 0:
                    sums[c, h] = bank([P, 2, CHUNK], f"sum{c}{h}", 2 * c + h)
                for s in range(2):
                    cols = slice(s * P, (s + 1) * P)
                    for tier in range(2):
                        w_codes, w_scales = tiers[a, h, tier]
                        nc.tensor.matmul_mx(
                            out=sums[c, h][:, s, :],
                            lhsT=w_codes[:, cols].bitcast(FP8X4),
                            lhsT_scale=w_scales[:, cols],
                            rhs=x_codes.bitcast(FP8X4),
                            rhs_scale=x_scales,
                            start=(a == 0 and s == 0 and tier == 0),
                            stop=(a == PASSES - 1 and s == 1 and tier == 1),
                        )

        def finish(c):
            total = sb([P, 2, 2, CHUNK], F32, f"total{c}", f"x_woven1{c + 1}" if c + 1 < CHUNKS else None)
            cols = slice(c * CHUNK, (c + 1) * CHUNK)
            for h in range(2):
                nc.vector.tensor_tensor(out=total[:, h], in0=sums[c, h][:], in1=residual[:, h, :, cols], op=ADD)
                rows = out[h * W_HALF : (h + 1) * W_HALF, cols]
                nc.sync.dma_start(out=rows.rearrange("(s p) j -> p s j", p=P), in_=total[:, h])

        for a in range(PASSES):
            for h in range(2):
                first_tier(a, h)
        second_tier(0, left_over(0, subtract_on_vector))
        late_woven = left_over(1, subtract_on_tensor)

        picked = sb([P, 2, PACK, J_HALF], F32, "picked0", "q_woven11")
        for i in range(PACK):
            for h in range(2):
                gather(picked[:, h], 0, i, h * J_HALF, J_HALF)
        for h in range(2):
            codes, scales = quantize_x(picked[:, h], J_HALF, f"0{h}")
            for s in range(2):
                cols = slice(s * CHUNK, (s + 1) * CHUNK)
                multiply(0, 2 * h + s, codes[:, cols], scales[:, cols])
        second_tier(1, late_woven, "x_woven00")

        picked = sb([P, PACK, J_HALF], F32, "picked1")
        for i in range(PACK):
            gather(picked, 1, i, 0, J_HALF)
        for c in range(2):
            codes, scales = quantize_x(picked[:, :, c * CHUNK : (c + 1) * CHUNK], CHUNK, f"1{c}")
            multiply(1, c, codes[:], scales[:])
        for c, slot in ((2, "gate0"), (3, "x_woven10")):
            picked = sb([P, PACK, CHUNK], F32, f"picked1{c}", slot)
            for i in range(PACK):
                gather(picked, 1, i, c * CHUNK, CHUNK)
            codes, scales = quantize_x(picked[:], CHUNK, f"1{c}")
            multiply(1, c, codes[:], scales[:])
        for c in range(CHUNKS):
            finish(c)
